import numpy as np
CORES = [0,1,2,3]
N = 4
WIDTHS = [256,64,128,256]
XW = 256
def setup_inputs(rng):
    return {"x": rng.standard_normal((N, 128, XW), dtype=np.float32)}
def reference(x):
    g = np.concatenate([x[r][:, :WIDTHS[r]] for r in range(N)], axis=1)
    return {"y": np.broadcast_to(g, (N,) + g.shape)}

from concourse.bass import DstId, RemoteDMATransfer

SCRATCH = {
    "gath": ("sbuf", [128, 704], "float32"),
}
SEMAPHORES = ["loaded", "arrived", "sent", "stored"]

ENGINES = 16


def rank_program(g, core, T, topo):
    rank = T.rank_of(core)
    if rank is None:
        return

    widths = T.tables["WIDTHS"]
    off = [sum(widths[:r]) for r in range(len(widths))]
    lo, hi = off[rank], off[rank] + widths[rank]
    mine = T.gath[:, lo:hi]
    peers = [c for c in T.cores if c != core]

    g.sync.dma_start(mine, T.x[:, 0:widths[rank]]).then_inc(T.sem.loaded, 16)

    g.wait_ge(T.sem.loaded, 16)
    g.remote_dma_fused(
        [
            RemoteDMATransfer(
                dst_ids=[DstId(rid=topo.addr(p)[0], pnc=topo.addr(p)[1]) for p in peers],
                dma_engine_mask=topo.mask(core, peers[0]),
                remote_sem=T.sem.arrived,
                srcs=[mine],
                dsts=[mine for _p in peers],
            )
        ],
        local_sem=T.sem.sent,
    )

    g.sync.wait_ge(T.sem.loaded, 16)
    g.sync.wait_ge(T.sem.arrived, ENGINES * len(peers))
    g.sync.dma_start(T.y[:, :], T.gath[:, :]).then_inc(T.sem.stored, 16)
    g.sync.wait_ge(T.sem.stored, 16)

    g.wait_ge(T.sem.sent, ENGINES)
